import numpy as np
import ml_dtypes


def mxq(x, axis, fmt="e4m3"):
    dtype, down = {"e4m3": (ml_dtypes.float8_e4m3fn, 7), "e5m2": (ml_dtypes.float8_e5m2, 14)}[fmt]
    v = np.moveaxis(np.asarray(x, np.float32).astype(ml_dtypes.bfloat16).astype(np.float64), axis, -1)
    blocks = v.reshape(v.shape[:-1] + (-1, 32))
    amax = np.abs(blocks).max(-1, keepdims=True)
    byte = np.maximum(np.where(amax > 0, np.frexp(amax)[1] - 1 + 127, 0) - down, 1)
    scale = np.exp2(byte - 127.0)
    codes = (blocks / scale).astype(np.float32).astype(dtype).astype(np.float64)
    return np.moveaxis((codes * scale).reshape(v.shape), -1, axis)


WIDE = False


def mx_kscale(k):
    if not WIDE:
        return np.ones(k)
    levels = np.array([10, -10, 5, -5, 0])
    if k % 512:
        return np.exp2(np.random.permutation(np.resize(levels, k // 32))).repeat(32)
    a = np.empty((k // 512, 16))
    for p in range(k // 512):
        a[p, :8] = np.random.permutation(np.resize(levels, 8))
        for g in range(8):
            far = levels[np.abs(levels - a[p, g]) >= 10]
            a[p, g + 8] = far[np.random.randint(len(far))]
    return np.exp2(a.ravel()).repeat(32)


def f64(x):
    return np.asarray(x).astype(np.float64)


def striped(idx):
    return np.tile(idx.reshape(-1, 16).T, (8, 1)).astype(np.uint16)


def unstriped(offs):
    return offs[:16].T.reshape(-1).astype(np.int64)


def pack_weight(w):
    k, n = w.shape
    w = f64(np.asarray(w, np.float32).astype(ml_dtypes.bfloat16)).reshape(k // 32, 32, n)
    amax = np.abs(w).max(1)
    byte = np.clip(np.where(amax > 0, np.frexp(amax)[1] - 1 + 127 - 7, 1), 1, 254)
    scaled = (w * np.exp2(127.0 - byte)[:, None, :]).reshape(k, n).astype(np.float32)
    words = np.ascontiguousarray(scaled.reshape(k // 512, 128, 4, n).transpose(0, 1, 3, 2)).astype(ml_dtypes.float8_e4m3fn).view(np.uint8)
    return words, np.ascontiguousarray(byte.astype(np.uint8).reshape(k // 512, 16, n))


def unpack_weight(words, scales):
    g, p, n, _ = words.shape
    vals = np.ascontiguousarray(words).view(ml_dtypes.float8_e4m3fn).astype(np.float64) * np.repeat(np.exp2(scales.astype(np.float64) - 127.0), 8, axis=1)[..., None]
    return vals.transpose(0, 1, 3, 2).reshape(g * 512, n)


K, T, S, D, N, U = 1024, 1024, 512, 2, 128, 1024


def setup_inputs():
    n = np.random.standard_normal
    s = mx_kscale(K)[:, None]
    packed_xT = pack_weight(n((K, T)) * s)
    return {
        "x_words": packed_xT[0],
        "x_scales": packed_xT[1],
        "w1": (n((K, N)) / np.sqrt(K) / s).astype(np.float32),
        "avg": (np.random.uniform(0.3, 2.0, (N, U))).astype(np.float32),
        "offs": striped(np.random.permutation(T)[:S]),
        "usr": striped(np.random.permutation(U)[:S]),
    }


def reference(x_words, x_scales, w1, avg, offs, usr):
    xq = unpack_weight(x_words, x_scales)[:, unstriped(offs)]
    y = mxq(f64(w1), 0, "e4m3").T @ xq
    rate = np.log(np.exp(y) + 1.0)
    ag = f64(avg)[:, unstriped(usr)]
    met = rate / ag
    m3 = 3.0 * met
    top = m3.reshape(len(m3), -1, D).max(axis=2)
    ex = np.exp(m3 - np.repeat(top, D, axis=1))
    total = ex.reshape(len(ex), -1, D).sum(axis=2)
    share = ex / np.repeat(total, D, axis=1)
    na = 0.8 * ag + 0.2 * (share * rate)
    ut = share * np.log(na)
    return ut.reshape(len(ut), -1, D).sum(axis=2) + 0.1 * (met.reshape(len(met), -1, D).max(axis=2))

@@ -1,0 +1,148 @@
+from contextlib import ExitStack
+
+import concourse.mybir as mybir
+
+K, T, S, N, U = 1024, 1024, 512, 128, 1024
+FLOPS = 2 * K * N * S
+
+F32 = mybir.dt.float32
+BF16 = mybir.dt.bfloat16
+I32 = mybir.dt.int32
+U32 = mybir.dt.uint32
+U16 = mybir.dt.uint16
+U8 = mybir.dt.uint8
+FP8X4 = mybir.dt.float8_e4m3fn_x4
+ALU = mybir.AluOpType
+ACT = mybir.ActivationFunctionType
+
+P = 128
+PACK = 4
+PASSES = K // (P * PACK)
+HALVES = 2
+ENT = S // HALVES
+RES = ENT // 2
+COLS = ENT // 16
+
+
+def tile_picked_ypf_worth_p_kernel(tc, x_words, x_scales, w1, avg, offs, usr, out):
+    nc = tc.nc
+    halves = range(HALVES)
+    with ExitStack() as ctx:
+        sb = ctx.enter_context(tc.tile_pool(name="sb", bufs=1))
+        psum = ctx.enter_context(tc.psum_pool(name="psum", bufs=1))
+
+        def tiles(name, shape, dtype, count):
+            return [sb.tile(shape, dtype, name="%s%d" % (name, i), align_bytes=64) for i in range(count)]
+
+        offs_sb = sb.tile([P, S // 16], U16, name="offs_sb")
+        usr_sb = sb.tile([P, S // 16], U16, name="usr_sb")
+        scale_table = sb.tile([P, T], U8, name="scale_table", align_bytes=64)
+        word_table = tiles("word_table", [P, T], U32, PASSES)
+        w_raw = tiles("w_raw", [P, PACK, N], F32, PASSES)
+        avg_table = sb.tile([P, U], F32, name="avg_table")
+
+        nc.vector.memset(scale_table[:].bitcast(I32), 0)
+        nc.sync.dma_start(offs_sb[:], offs)
+        nc.sync.dma_start(word_table[0][:].bitcast(I32), x_words[0].rearrange("p n t -> p (n t)").bitcast(I32))
+        for q in range(4):
+            nc.sync.dma_start(scale_table[32 * q:32 * q + 4 * PASSES, :].bitcast(I32),
+                              x_scales[:, 4 * q:4 * q + 4, :].bitcast(I32))
+        for o in range(PASSES):
+            nc.sync.dma_start(w_raw[o][:], w1[o * P * PACK:(o + 1) * P * PACK, :].rearrange("(p j) m -> p j m", j=PACK))
+        nc.sync.dma_start(word_table[1][:].bitcast(I32), x_words[1].rearrange("p n t -> p (n t)").bitcast(I32))
+        nc.sync.dma_start(avg_table[:], avg)
+        nc.sync.dma_start(usr_sb[:], usr)
+
+        x_sc = sb.tile([P, S], U8, name="x_sc", align_bytes=64)
+        nc.vector.tensor_copy(x_sc[:], scale_table[:].indirect(offs_sb[:]))
+
+        w_bf = sb.tile([P, PASSES, N, PACK], BF16, name="w_bf", tag="staging", align_bytes=64)
+        w_codes = sb.tile([P, PASSES, N], U32, name="w_codes", align_bytes=64)
+        w_sc = sb.tile([P, PASSES, N], U8, name="w_sc", align_bytes=64)
+        first = tiles("first", [P, ENT], U32, HALVES)
+        y = [psum.tile([P, ENT], F32, name="y%d" % h) for h in halves]
+        for o in range(PASSES):
+            nc.scalar.copy(w_bf[:, o], w_raw[o][:].rearrange("p j m -> p m j"))
+        for h in halves:
+            nc.vector.tensor_copy(first[h][:], word_table[0][:].indirect(offs_sb[:, h * COLS:(h + 1) * COLS]))
+        nc.vector.quantize_mx(out=w_codes[:].rearrange("p o m -> p (o m)").bitcast(FP8X4),
+                              scales=w_sc[:].rearrange("p o m -> p (o m)"),
+                              in_=w_bf[:].rearrange("p o m j -> p (o m j)"))
+        second = sb.tile([P, HALVES, ENT], U32, name="second", tag="staging", align_bytes=64)
+        for h in halves:
+            nc.vector.tensor_copy(second[:, h, :], word_table[1][:].indirect(offs_sb[:, h * COLS:(h + 1) * COLS]))
+        x_codes = [[first[h][:] for h in halves], [second[:, h, :] for h in halves]]
+        for o in range(PASSES):
+            for h in halves:
+                nc.tensor.matmul_mx(out=y[h][:], lhsT=w_codes[:, o, :].bitcast(FP8X4), lhsT_scale=w_sc[:, o, :],
+                                    rhs=x_codes[o][h].bitcast(FP8X4),
+                                    rhs_scale=x_sc[4 * o:P, h * ENT:(h + 1) * ENT],
+                                    start=(o == 0), stop=(o == PASSES - 1))
+
+        def planes(ap):
+            return ap.rearrange("p (v d) -> p d v", d=2)
+
+        mag = tiles("mag", [P, 2, RES], F32, HALVES)
+        decay = tiles("decay", [P, 2, RES], F32, HALVES)
+        soft = tiles("soft", [P, 2, RES], F32, HALVES)
+        for h in halves:
+            nc.scalar.activation(mag[h][:], planes(y[h][:]), ACT.Abs)
+            nc.scalar.activation(decay[h][:], mag[h][:], ACT.Exp, scale=-1.0)
+
+        ag = tiles("ag", [P, ENT], F32, HALVES)
+        prod = tiles("prod", [P, RES], F32, HALVES)
+        iprod = tiles("iprod", [P, RES], F32, HALVES)
+        for h in halves:
+            nc.vector.tensor_copy(ag[h][:], avg_table[:].indirect(usr_sb[:, h * COLS:(h + 1) * COLS]))
+        for h in halves:
+            nc.vector.tensor_tensor(prod[h][:], planes(ag[h][:])[:, 0, :], planes(ag[h][:])[:, 1, :], ALU.mult)
+        for h in halves:
+            nc.vector.reciprocal(iprod[h][:], prod[h][:])
+
+        for h in halves:
+            nc.scalar.activation(soft[h][:], decay[h][:], ACT.Ln, bias=1.0)
+
+        rate = tiles("rate", [P, 2, RES], F32, HALVES)
+        met = tiles("met", [P, 2, RES], F32, HALVES)
+        gap = tiles("gap", [P, RES], F32, HALVES)
+        best = tiles("best", [P, RES], F32, HALVES)
+        share = tiles("share", [P, 2, RES], F32, HALVES)
+        for h in halves:
+            nc.vector.scalar_tensor_tensor(rate[h][:], planes(y[h][:]), 0.0, soft[h][:], ALU.max, ALU.add)
+        for h in halves:
+            nc.vector.tensor_tensor(met[h][:], rate[h][:], planes(ag[h][:])[:, ::-1, :], ALU.mult)
+        raw_gap = tiles("raw_gap", [P, RES], F32, HALVES)
+        raw_best = tiles("raw_best", [P, RES], F32, HALVES)
+        for h in halves:
+            nc.vector.tensor_tensor(raw_gap[h][:], met[h][:, 0, :], met[h][:, 1, :], ALU.subtract)
+        for h in halves:
+            nc.vector.tensor_tensor(gap[h][:], raw_gap[h][:], iprod[h][:], ALU.mult)
+        for h in halves:
+            nc.scalar.activation(share[h][:, 0, :], gap[h][:], ACT.Sigmoid, scale=3.0)
+        for h in halves:
+            nc.vector.tensor_tensor(raw_best[h][:], met[h][:, 0, :], met[h][:, 1, :], ALU.max)
+
+        got = tiles("got", [P, 2, RES], F32, HALVES)
+        mix = tiles("mix", [P, 2, RES], F32, HALVES)
+        lg = tiles("lg", [P, 2, RES], F32, HALVES)
+        for h in halves:
+            nc.vector.tensor_scalar(share[h][:, 1, :], share[h][:, 0, :], -1.0, 1.0, ALU.mult, ALU.add)
+        for h in halves:
+            nc.vector.tensor_tensor(got[h][:], share[h][:], rate[h][:], ALU.mult)
+        for h in halves:
+            nc.vector.scalar_tensor_tensor(mix[h][:], got[h][:], 0.25, planes(ag[h][:]), ALU.mult, ALU.add)
+        for h in halves:
+            nc.scalar.activation(lg[h][:], mix[h][:], ACT.Ln, scale=0.8)
+        for h in halves:
+            nc.vector.tensor_tensor(best[h][:], raw_best[h][:], iprod[h][:], ALU.mult)
+
+        ut = tiles("ut", [P, 2, RES], F32, HALVES)
+        part = tiles("part", [P, RES], F32, HALVES)
+        res = tiles("res", [P, RES], F32, HALVES)
+        for h in halves:
+            nc.vector.tensor_tensor(ut[h][:], share[h][:], lg[h][:], ALU.mult)
+        for h in halves:
+            nc.vector.scalar_tensor_tensor(part[h][:], best[h][:], 0.1, ut[h][:, 0, :], ALU.mult, ALU.add)
+        for h in halves:
+            nc.vector.tensor_tensor(res[h][:], part[h][:], ut[h][:, 1, :], ALU.add)
+            nc.sync.dma_start(out[:, h * RES:(h + 1) * RES], res[h][:])

@@ -37,7 +37,7 @@ def tile_picked_ypf_worth_p_kernel(tc, x_words, x_scales, w1, avg, offs, usr, ou
         offs_sb = sb.tile([P, S // 16], U16, name="offs_sb")
         usr_sb = sb.tile([P, S // 16], U16, name="usr_sb")
         scale_table = sb.tile([P, T], U8, name="scale_table", align_bytes=64)
-        word_table = tiles("word_table", [P, T], U32, PASSES)
+        word_table = [sb.tile([P, T], U32, name="word_table%d" % o, tag="table%d" % o, align_bytes=64) for o in range(PASSES)]
         w_raw = tiles("w_raw", [P, PACK, N], F32, PASSES)
         avg_table = sb.tile([P, U], F32, name="avg_table")
 
@@ -59,19 +59,18 @@ def tile_picked_ypf_worth_p_kernel(tc, x_words, x_scales, w1, avg, offs, usr, ou
         w_bf = sb.tile([P, PASSES, N, PACK], BF16, name="w_bf", tag="staging", align_bytes=64)
         w_codes = sb.tile([P, PASSES, N], U32, name="w_codes", align_bytes=64)
         w_sc = sb.tile([P, PASSES, N], U8, name="w_sc", align_bytes=64)
-        first = tiles("first", [P, ENT], U32, HALVES)
+        first = sb.tile([P, S], U32, name="first", align_bytes=64)
         y = [psum.tile([P, ENT], F32, name="y%d" % h) for h in halves]
         for o in range(PASSES):
             nc.scalar.copy(w_bf[:, o], w_raw[o][:].rearrange("p j m -> p m j"))
-        for h in halves:
-            nc.vector.tensor_copy(first[h][:], word_table[0][:].indirect(offs_sb[:, h * COLS:(h + 1) * COLS]))
+        nc.vector.tensor_copy(first[:], word_table[0][:].indirect(offs_sb[:]))
         nc.vector.quantize_mx(out=w_codes[:].rearrange("p o m -> p (o m)").bitcast(FP8X4),
                               scales=w_sc[:].rearrange("p o m -> p (o m)"),
                               in_=w_bf[:].rearrange("p o m j -> p (o m j)"))
         second = sb.tile([P, HALVES, ENT], U32, name="second", tag="staging", align_bytes=64)
         for h in halves:
             nc.vector.tensor_copy(second[:, h, :], word_table[1][:].indirect(offs_sb[:, h * COLS:(h + 1) * COLS]))
-        x_codes = [[first[h][:] for h in halves], [second[:, h, :] for h in halves]]
+        x_codes = [[first[:, h * ENT:(h + 1) * ENT] for h in halves], [second[:, h, :] for h in halves]]
         for o in range(PASSES):
             for h in halves:
                 nc.tensor.matmul_mx(out=y[h][:], lhsT=w_codes[:, o, :].bitcast(FP8X4), lhsT_scale=w_sc[:, o, :],
@@ -89,60 +88,60 @@ def tile_picked_ypf_worth_p_kernel(tc, x_words, x_scales, w1, avg, offs, usr, ou
             nc.scalar.activation(mag[h][:], planes(y[h][:]), ACT.Abs)
             nc.scalar.activation(decay[h][:], mag[h][:], ACT.Exp, scale=-1.0)
 
-        ag = tiles("ag", [P, ENT], F32, HALVES)
+        ag_all = sb.tile([P, HALVES, ENT], F32, name="ag_all", tag="table1", align_bytes=64)
+        ag = [ag_all[:, h, :] for h in halves]
         prod = tiles("prod", [P, RES], F32, HALVES)
         iprod = tiles("iprod", [P, RES], F32, HALVES)
         for h in halves:
-            nc.vector.tensor_copy(ag[h][:], avg_table[:].indirect(usr_sb[:, h * COLS:(h + 1) * COLS]))
-        for h in halves:
-            nc.vector.tensor_tensor(prod[h][:], planes(ag[h][:])[:, 0, :], planes(ag[h][:])[:, 1, :], ALU.mult)
+            nc.vector.tensor_copy(ag[h], avg_table[:].indirect(usr_sb[:, h * COLS:(h + 1) * COLS]))
+        inv = tiles("inv", [P, 2, RES], F32, HALVES)
+        for h, eng in enumerate((nc.vector, nc.gpsimd)):
+            eng.tensor_tensor(prod[h][:], planes(ag[h])[:, 0, :], planes(ag[h])[:, 1, :], ALU.mult)
         for h in halves:
             nc.vector.reciprocal(iprod[h][:], prod[h][:])
+        for h, eng in enumerate((nc.gpsimd, nc.gpsimd)):
+            eng.tensor_tensor(inv[h][:], planes(ag[h])[:, ::-1, :],
+                              iprod[h][:].unsqueeze(1).broadcast_to([P, 2, RES]), ALU.mult)
 
         for h in halves:
             nc.scalar.activation(soft[h][:], decay[h][:], ACT.Ln, bias=1.0)
 
-        rate = tiles("rate", [P, 2, RES], F32, HALVES)
+        def wide(name, shape):
+            return sb.tile([P] + shape, F32, name=name, align_bytes=64)
+
+        rate = wide("rate", [HALVES, 2, RES])
         met = tiles("met", [P, 2, RES], F32, HALVES)
         gap = tiles("gap", [P, RES], F32, HALVES)
-        best = tiles("best", [P, RES], F32, HALVES)
-        share = tiles("share", [P, 2, RES], F32, HALVES)
+        best = wide("best", [HALVES, RES])
+        share = wide("share", [HALVES, RES])
         for h in halves:
-            nc.vector.scalar_tensor_tensor(rate[h][:], planes(y[h][:]), 0.0, soft[h][:], ALU.max, ALU.add)
+            nc.vector.scalar_tensor_tensor(rate[:, h], planes(y[h][:]), 0.0, soft[h][:], ALU.max, ALU.add)
         for h in halves:
-            nc.vector.tensor_tensor(met[h][:], rate[h][:], planes(ag[h][:])[:, ::-1, :], ALU.mult)
-        raw_gap = tiles("raw_gap", [P, RES], F32, HALVES)
-        raw_best = tiles("raw_best", [P, RES], F32, HALVES)
+            nc.vector.tensor_tensor(met[h][:], rate[:, h], inv[h][:], ALU.mult)
         for h in halves:
-            nc.vector.tensor_tensor(raw_gap[h][:], met[h][:, 0, :], met[h][:, 1, :], ALU.subtract)
+            nc.vector.tensor_tensor(gap[h][:], met[h][:, 0, :], met[h][:, 1, :], ALU.subtract)
         for h in halves:
-            nc.vector.tensor_tensor(gap[h][:], raw_gap[h][:], iprod[h][:], ALU.mult)
+            nc.scalar.activation(share[:, h], gap[h][:], ACT.Sigmoid, scale=3.0)
         for h in halves:
-            nc.scalar.activation(share[h][:, 0, :], gap[h][:], ACT.Sigmoid, scale=3.0)
-        for h in halves:
-            nc.vector.tensor_tensor(raw_best[h][:], met[h][:, 0, :], met[h][:, 1, :], ALU.max)
+            nc.vector.tensor_tensor(best[:, h], met[h][:, 0, :], met[h][:, 1, :], ALU.max)
 
-        got = tiles("got", [P, 2, RES], F32, HALVES)
-        mix = tiles("mix", [P, 2, RES], F32, HALVES)
-        lg = tiles("lg", [P, 2, RES], F32, HALVES)
-        for h in halves:
-            nc.vector.tensor_scalar(share[h][:, 1, :], share[h][:, 0, :], -1.0, 1.0, ALU.mult, ALU.add)
-        for h in halves:
-            nc.vector.tensor_tensor(got[h][:], share[h][:], rate[h][:], ALU.mult)
-        for h in halves:
-            nc.vector.scalar_tensor_tensor(mix[h][:], got[h][:], 0.25, planes(ag[h][:]), ALU.mult, ALU.add)
-        for h in halves:
-            nc.scalar.activation(lg[h][:], mix[h][:], ACT.Ln, scale=0.8)
-        for h in halves:
-            nc.vector.tensor_tensor(best[h][:], raw_best[h][:], iprod[h][:], ALU.mult)
-
-        ut = tiles("ut", [P, 2, RES], F32, HALVES)
-        part = tiles("part", [P, RES], F32, HALVES)
+        ag_plane = ag_all[:].rearrange("p h (v d) -> p d h v", d=2)
+        got = [wide("got%d" % d, [HALVES, RES]) for d in range(2)]
+        mix = [wide("mix%d" % d, [HALVES, RES]) for d in range(2)]
+        lg = [wide("lg%d" % d, [HALVES, RES]) for d in range(2)]
+        ut = [wide("ut%d" % d, [HALVES, RES]) for d in range(2)]
+        part = wide("part", [HALVES, RES])
         res = tiles("res", [P, RES], F32, HALVES)
+        nc.vector.scalar_tensor_tensor(got[1][:], share[:], 1.0, rate[:, :, 1, :], ALU.subtract, ALU.mult)
+        nc.vector.tensor_tensor(got[0][:], share[:], rate[:, :, 0, :], ALU.mult)
+        nc.vector.scalar_tensor_tensor(mix[1][:], got[1][:], 0.25, ag_plane[:, 1], ALU.mult, ALU.subtract)
+        nc.vector.scalar_tensor_tensor(mix[0][:], got[0][:], 0.25, ag_plane[:, 0], ALU.mult, ALU.add)
+        nc.scalar.activation(lg[1][:], mix[1][:], ACT.Ln, scale=-0.8)
+        nc.scalar.activation(lg[0][:], mix[0][:], ACT.Ln, scale=0.8)
+        nc.vector.scalar_tensor_tensor(ut[1][:], share[:], 1.0, lg[1][:], ALU.subtract, ALU.mult)
+        nc.vector.tensor_tensor(ut[0][:], share[:], lg[0][:], ALU.mult)
         for h in halves:
-            nc.vector.tensor_tensor(ut[h][:], share[h][:], lg[h][:], ALU.mult)
+            nc.vector.scalar_tensor_tensor(part[:, h], best[:, h], 0.1, ut[1][:, h], ALU.mult, ALU.subtract)
         for h in halves:
-            nc.vector.scalar_tensor_tensor(part[h][:], best[h][:], 0.1, ut[h][:, 0, :], ALU.mult, ALU.add)
-        for h in halves:
-            nc.vector.tensor_tensor(res[h][:], part[h][:], ut[h][:, 1, :], ALU.add)
+            nc.vector.tensor_tensor(res[h][:], part[:, h], ut[0][:, h], ALU.add)
             nc.sync.dma_start(out[:, h * RES:(h + 1) * RES], res[h][:])

from contextlib import ExitStack

import concourse.mybir as mybir

K, T, S, N, U = 1024, 1024, 512, 128, 1024
FLOPS = 2 * K * N * S

F32 = mybir.dt.float32
BF16 = mybir.dt.bfloat16
I32 = mybir.dt.int32
U32 = mybir.dt.uint32
U16 = mybir.dt.uint16
U8 = mybir.dt.uint8
FP8X4 = mybir.dt.float8_e4m3fn_x4
ALU = mybir.AluOpType
ACT = mybir.ActivationFunctionType

P = 128
PACK = 4
PASSES = K // (P * PACK)
HALVES = 2
ENT = S // HALVES
RES = ENT // 2
COLS = ENT // 16


def tile_picked_ypf_worth_p_kernel(tc, x_words, x_scales, w1, avg, offs, usr, out):
    nc = tc.nc
    halves = range(HALVES)
    with ExitStack() as ctx:
        sb = ctx.enter_context(tc.tile_pool(name="sb", bufs=1))
        psum = ctx.enter_context(tc.psum_pool(name="psum", bufs=1))

        def tiles(name, shape, dtype, count):
            return [sb.tile(shape, dtype, name="%s%d" % (name, i), align_bytes=64) for i in range(count)]

        offs_sb = sb.tile([P, S // 16], U16, name="offs_sb")
        usr_sb = sb.tile([P, S // 16], U16, name="usr_sb")
        scale_table = sb.tile([P, T], U8, name="scale_table", align_bytes=64)
        word_table = [sb.tile([P, T], U32, name="word_table%d" % o, tag="table%d" % o, align_bytes=64) for o in range(PASSES)]
        w_raw = tiles("w_raw", [P, PACK, N], F32, PASSES)
        avg_table = sb.tile([P, U], F32, name="avg_table")

        nc.vector.memset(scale_table[:].bitcast(I32), 0)
        nc.sync.dma_start(offs_sb[:], offs)
        nc.sync.dma_start(word_table[0][:].bitcast(I32), x_words[0].rearrange("p n t -> p (n t)").bitcast(I32))
        for q in range(4):
            nc.sync.dma_start(scale_table[32 * q:32 * q + 4 * PASSES, :].bitcast(I32),
                              x_scales[:, 4 * q:4 * q + 4, :].bitcast(I32))
        for o in range(PASSES):
            nc.sync.dma_start(w_raw[o][:], w1[o * P * PACK:(o + 1) * P * PACK, :].rearrange("(p j) m -> p j m", j=PACK))
        nc.sync.dma_start(word_table[1][:].bitcast(I32), x_words[1].rearrange("p n t -> p (n t)").bitcast(I32))
        nc.sync.dma_start(avg_table[:], avg)
        nc.sync.dma_start(usr_sb[:], usr)

        x_sc = sb.tile([P, S], U8, name="x_sc", align_bytes=64)
        nc.vector.tensor_copy(x_sc[:], scale_table[:].indirect(offs_sb[:]))

        w_bf = sb.tile([P, PASSES, N, PACK], BF16, name="w_bf", tag="staging", align_bytes=64)
        w_codes = sb.tile([P, PASSES, N], U32, name="w_codes", align_bytes=64)
        w_sc = sb.tile([P, PASSES, N], U8, name="w_sc", align_bytes=64)
        first = sb.tile([P, S], U32, name="first", align_bytes=64)
        y = [psum.tile([P, ENT], F32, name="y%d" % h) for h in halves]
        for o in range(PASSES):
            nc.scalar.copy(w_bf[:, o], w_raw[o][:].rearrange("p j m -> p m j"))
        nc.vector.tensor_copy(first[:], word_table[0][:].indirect(offs_sb[:]))
        nc.vector.quantize_mx(out=w_codes[:].rearrange("p o m -> p (o m)").bitcast(FP8X4),
                              scales=w_sc[:].rearrange("p o m -> p (o m)"),
                              in_=w_bf[:].rearrange("p o m j -> p (o m j)"))
        second = sb.tile([P, HALVES, ENT], U32, name="second", tag="staging", align_bytes=64)
        for h in halves:
            nc.vector.tensor_copy(second[:, h, :], word_table[1][:].indirect(offs_sb[:, h * COLS:(h + 1) * COLS]))
        x_codes = [[first[:, h * ENT:(h + 1) * ENT] for h in halves], [second[:, h, :] for h in halves]]
        for o in range(PASSES):
            for h in halves:
                nc.tensor.matmul_mx(out=y[h][:], lhsT=w_codes[:, o, :].bitcast(FP8X4), lhsT_scale=w_sc[:, o, :],
                                    rhs=x_codes[o][h].bitcast(FP8X4),
                                    rhs_scale=x_sc[4 * o:P, h * ENT:(h + 1) * ENT],
                                    start=(o == 0), stop=(o == PASSES - 1))

        def planes(ap):
            return ap.rearrange("p (v d) -> p d v", d=2)

        mag = tiles("mag", [P, 2, RES], F32, HALVES)
        decay = tiles("decay", [P, 2, RES], F32, HALVES)
        soft = tiles("soft", [P, 2, RES], F32, HALVES)
        for h in halves:
            nc.scalar.activation(mag[h][:], planes(y[h][:]), ACT.Abs)
            nc.scalar.activation(decay[h][:], mag[h][:], ACT.Exp, scale=-1.0)

        ag_all = sb.tile([P, HALVES, ENT], F32, name="ag_all", tag="table1", align_bytes=64)
        ag = [ag_all[:, h, :] for h in halves]
        prod = tiles("prod", [P, RES], F32, HALVES)
        iprod = tiles("iprod", [P, RES], F32, HALVES)
        for h in halves:
            nc.vector.tensor_copy(ag[h], avg_table[:].indirect(usr_sb[:, h * COLS:(h + 1) * COLS]))
        inv = tiles("inv", [P, 2, RES], F32, HALVES)
        for h, eng in enumerate((nc.vector, nc.gpsimd)):
            eng.tensor_tensor(prod[h][:], planes(ag[h])[:, 0, :], planes(ag[h])[:, 1, :], ALU.mult)
        for h in halves:
            nc.vector.reciprocal(iprod[h][:], prod[h][:])
        for h, eng in enumerate((nc.gpsimd, nc.gpsimd)):
            eng.tensor_tensor(inv[h][:], planes(ag[h])[:, ::-1, :],
                              iprod[h][:].unsqueeze(1).broadcast_to([P, 2, RES]), ALU.mult)

        for h in halves:
            nc.scalar.activation(soft[h][:], decay[h][:], ACT.Ln, bias=1.0)

        def wide(name, shape):
            return sb.tile([P] + shape, F32, name=name, align_bytes=64)

        rate = wide("rate", [HALVES, 2, RES])
        met = tiles("met", [P, 2, RES], F32, HALVES)
        gap = tiles("gap", [P, RES], F32, HALVES)
        best = wide("best", [HALVES, RES])
        share = wide("share", [HALVES, RES])
        for h in halves:
            nc.vector.scalar_tensor_tensor(rate[:, h], planes(y[h][:]), 0.0, soft[h][:], ALU.max, ALU.add)
        for h in halves:
            nc.vector.tensor_tensor(met[h][:], rate[:, h], inv[h][:], ALU.mult)
        for h in halves:
            nc.vector.tensor_tensor(gap[h][:], met[h][:, 0, :], met[h][:, 1, :], ALU.subtract)
        for h in halves:
            nc.scalar.activation(share[:, h], gap[h][:], ACT.Sigmoid, scale=3.0)
        for h in halves:
            nc.vector.tensor_tensor(best[:, h], met[h][:, 0, :], met[h][:, 1, :], ALU.max)

        ag_plane = ag_all[:].rearrange("p h (v d) -> p d h v", d=2)
        got = [wide("got%d" % d, [HALVES, RES]) for d in range(2)]
        mix = [wide("mix%d" % d, [HALVES, RES]) for d in range(2)]
        lg = [wide("lg%d" % d, [HALVES, RES]) for d in range(2)]
        ut = [wide("ut%d" % d, [HALVES, RES]) for d in range(2)]
        part = wide("part", [HALVES, RES])
        res = tiles("res", [P, RES], F32, HALVES)
        nc.vector.scalar_tensor_tensor(got[1][:], share[:], 1.0, rate[:, :, 1, :], ALU.subtract, ALU.mult)
        nc.vector.tensor_tensor(got[0][:], share[:], rate[:, :, 0, :], ALU.mult)
        nc.vector.scalar_tensor_tensor(mix[1][:], got[1][:], 0.25, ag_plane[:, 1], ALU.mult, ALU.subtract)
        nc.vector.scalar_tensor_tensor(mix[0][:], got[0][:], 0.25, ag_plane[:, 0], ALU.mult, ALU.add)
        nc.scalar.activation(lg[1][:], mix[1][:], ACT.Ln, scale=-0.8)
        nc.scalar.activation(lg[0][:], mix[0][:], ACT.Ln, scale=0.8)
        nc.vector.scalar_tensor_tensor(ut[1][:], share[:], 1.0, lg[1][:], ALU.subtract, ALU.mult)
        nc.vector.tensor_tensor(ut[0][:], share[:], lg[0][:], ALU.mult)
        for h in halves:
            nc.vector.scalar_tensor_tensor(part[:, h], best[:, h], 0.1, ut[1][:, h], ALU.mult, ALU.subtract)
        for h in halves:
            nc.vector.tensor_tensor(res[h][:], part[:, h], ut[0][:, h], ALU.add)
            nc.sync.dma_start(out[:, h * RES:(h + 1) * RES], res[h][:])
